import numpy as np
import ml_dtypes


def mxq(x, axis, fmt="e4m3"):
    dtype, down = {"e4m3": (ml_dtypes.float8_e4m3fn, 7), "e5m2": (ml_dtypes.float8_e5m2, 14)}[fmt]
    v = np.moveaxis(np.asarray(x, np.float32).astype(ml_dtypes.bfloat16).astype(np.float64), axis, -1)
    blocks = v.reshape(v.shape[:-1] + (-1, 32))
    amax = np.abs(blocks).max(-1, keepdims=True)
    byte = np.maximum(np.where(amax > 0, np.frexp(amax)[1] - 1 + 127, 0) - down, 1)
    scale = np.exp2(byte - 127.0)
    codes = (blocks / scale).astype(np.float32).astype(dtype).astype(np.float64)
    return np.moveaxis((codes * scale).reshape(v.shape), -1, axis)


WIDE = False


def mx_kscale(k):
    if not WIDE:
        return np.ones(k)
    levels = np.array([10, -10, 5, -5, 0])
    if k % 512:
        return np.exp2(np.random.permutation(np.resize(levels, k // 32))).repeat(32)
    a = np.empty((k // 512, 16))
    for p in range(k // 512):
        a[p, :8] = np.random.permutation(np.resize(levels, 8))
        for g in range(8):
            far = levels[np.abs(levels - a[p, g]) >= 10]
            a[p, g + 8] = far[np.random.randint(len(far))]
    return np.exp2(a.ravel()).repeat(32)


def f64(x):
    return np.asarray(x).astype(np.float64)


def striped(idx):
    return np.tile(idx.reshape(-1, 16).T, (8, 1)).astype(np.uint16)


def unstriped(offs):
    return offs[:16].T.reshape(-1).astype(np.int64)


E2M1 = np.array([0.0, 0.5, 1.0, 1.5, 2.0, 3.0, 4.0, 6.0, -0.0, -0.5, -1.0, -1.5, -2.0, -3.0, -4.0, -6.0])


def pack_weight(w, fmt):
    k, n = w.shape
    w = f64(np.asarray(w, np.float32).astype(ml_dtypes.bfloat16)).reshape(k // 32, 32, n)
    amax = np.abs(w).max(1)
    if fmt == "e4m3":
        byte = np.frexp(amax)[1] - 1 + 127 - 7
    else:
        mant, ex = np.frexp(amax / 6.0)
        byte = np.where(mant > 0.5, ex, ex - 1) + 127
    byte = np.clip(np.where(amax > 0, byte, 1), 1, 254)
    scaled = (w * np.exp2(127.0 - byte)[:, None, :]).reshape(k, n).astype(np.float32)
    by_word = np.ascontiguousarray(scaled.reshape(k // 512, 128, 4, n).transpose(0, 1, 3, 2))
    if fmt == "e4m3":
        words = by_word.astype(ml_dtypes.float8_e4m3fn).view(np.uint8)
    else:
        c = by_word.astype(ml_dtypes.float4_e2m1fn).view(np.uint8) & 0xF
        words = (c[..., 0::2] | (c[..., 1::2] << 4)).reshape(k // 512, 128, 2 * n)
    return np.ascontiguousarray(words), np.ascontiguousarray(byte.astype(np.uint8).reshape(k // 512, 16, n))


def unpack_weight(words, scales, fmt):
    g, _, n = scales.shape
    words = np.ascontiguousarray(words).reshape(g, 128, n, -1)
    if fmt == "e4m3":
        vals = words.view(ml_dtypes.float8_e4m3fn).astype(np.float64)
    else:
        nib = np.empty((g, 128, n, 4), np.uint8)
        nib[..., 0::2] = words & 0xF
        nib[..., 1::2] = words >> 4
        vals = E2M1[nib]
    vals = vals * np.repeat(np.exp2(scales.astype(np.float64) - 127.0), 8, axis=1)[..., None]
    return vals.transpose(0, 1, 3, 2).reshape(g * 512, n)


def gelu(v):
    return 0.5 * v * (1.0 + np.tanh(np.sqrt(2.0 / np.pi) * (v + 0.044715 * v**3)))


K, T, S, P, H, N = 1024, 4096, 1024, 512, 1536, 384

def setup_inputs():
    n = np.random.standard_normal
    s = mx_kscale(K)[:, None]
    u = mx_kscale(H)[:, None]
    tab_words, tab_scales = pack_weight(n((K, T)) * s, "e4m3")
    wsp_words, wsp_scales = pack_weight(n((H, N)) / np.sqrt(H) / u, "e2m1")
    return {
        "tab_words": tab_words,
        "tab_scales": tab_scales,
        "offs": striped(np.random.permutation(T)[:S]),
        "pos1": striped(np.random.permutation(S)[:P]),
        "pos2": striped(np.random.permutation(S)[:P]),
        "w1": (n((K, H)) / np.sqrt(K) / s).astype(np.float32),
        "gain": (np.exp(0.4 * n(H)) * u[:, 0]).astype(np.float32),
        "slope": (1.4 * np.exp(0.2 * n(H)) / u[:, 0]).astype(np.float32),
        "bend": (1.5 * np.exp(0.3 * n(H)) * u[:, 0]).astype(np.float32),
        "hipm": (1.3 * n((H, P))).astype(np.float32),
        "wsp_words": wsp_words,
        "wsp_scales": wsp_scales,
        "whip": (1.2 * n((H, N)) / np.sqrt(H) / u).astype(np.float32),
        "shift": n(N).astype(np.float32),
    }

def reference(tab_words, tab_scales, offs, pos1, pos2, w1, gain, slope, bend, hipm, wsp_words, wsp_scales, whip, shift):
    v = unpack_weight(tab_words, tab_scales, "e4m3")[:, unstriped(offs)]
    h = f64(gain)[:, None] * (mxq(f64(w1), 0, "e4m3").T @ v)
    sp = h[:, unstriped(pos1)]
    xa = sp + f64(bend)[:, None] * np.tanh(f64(slope)[:, None] * sp)
    xb = h[:, unstriped(pos2)] * f64(hipm)
    wsp = unpack_weight(wsp_words, wsp_scales, "e2m1")
    y = wsp.T @ mxq(xa, 0, "e4m3") + mxq(f64(whip), 0, "e4m3").T @ mxq(xb, 0, "e4m3")
    return y + f64(shift)[:, None]

@@ -1,0 +1,269 @@
+from contextlib import ExitStack
+
+import concourse.mybir as mybir
+
+K, T, S, PAIRS, H, N = 1024, 4096, 1024, 512, 1536, 384
+FLOPS = 2 * K * H * S + 2 * 2 * H * N * PAIRS
+
+F32 = mybir.dt.float32
+BF16 = mybir.dt.bfloat16
+I32 = mybir.dt.int32
+U32 = mybir.dt.uint32
+U16 = mybir.dt.uint16
+U8 = mybir.dt.uint8
+FP8X4 = mybir.dt.float8_e4m3fn_x4
+FP4X4 = mybir.dt.float4_e2m1fn_x4
+MULT = mybir.AluOpType.mult
+ADD = mybir.AluOpType.add
+ACT = mybir.ActivationFunctionType
+
+P = 128
+PACK = 4
+PASS = P * PACK
+BANK = 512
+K_PASSES = K // PASS
+R_PASSES = H // PASS
+N_TILES = N // P
+QUADS = 4
+
+
+def tile_list_spine_hip_scores_kernel(
+    tc, tab_words, tab_scales, offs, pos1, pos2, w1, gain, slope, bend, hipm, wsp_words, wsp_scales, whip, shift, out
+):
+    nc = tc.nc
+    with ExitStack() as ctx:
+        keep = ctx.enter_context(tc.tile_pool(name="keep", bufs=1))
+        ring = ctx.enter_context(tc.tile_pool(name="ring", bufs=2))
+        psum = ctx.enter_context(tc.psum_pool(name="psum", bufs=1))
+
+        tab_plane = keep.tile([P, T], U8, name="tab_plane", align_bytes=64)
+        wsp_plane = keep.tile([P, R_PASSES, N], U8, name="wsp_plane", align_bytes=64)
+        nc.vector.memset(tab_plane[:].bitcast(I32), 0)
+        nc.vector.memset(wsp_plane[:].rearrange("p a n -> p (a n)").bitcast(I32), 0)
+
+        idx = keep.tile([P, S // 16], U16, name="idx")
+        p1 = keep.tile([P, PAIRS // 16], U16, name="p1")
+        p2 = keep.tile([P, PAIRS // 16], U16, name="p2")
+        tab = [keep.tile([P, T], U32, name=f"tab{g}") for g in range(K_PASSES)]
+        w1_raw = {}
+        hip = {}
+        whip_raw = {}
+
+        def load_w1(a, g, parts=1):
+            width = PASS // parts
+            raw = ring.tile([P, parts, PACK, width], F32, name="raw", tag="raw", bufs=4)
+            w1_raw[(a, g)] = raw
+            for u in range(parts):
+                c0 = a * PASS + u * width
+                nc.sync.dma_start(
+                    out=raw[:, u],
+                    in_=w1[g * PASS : (g + 1) * PASS, c0 : c0 + width].rearrange("(p j) c -> p j c", j=PACK),
+                )
+
+        def load_hip(a):
+            hip[a] = keep.tile([P, PACK, PAIRS], F32, name=f"hip{a}")
+            nc.sync.dma_start(out=hip[a][:], in_=hipm[a * PASS : (a + 1) * PASS].rearrange("(p t) j -> p t j", t=PACK))
+
+        def load_whip(a):
+            whip_raw[a] = ring.tile([P, PACK, N], F32, name="raw", tag="raw", bufs=4)
+            nc.sync.dma_start(out=whip_raw[a][:], in_=whip[a * PASS : (a + 1) * PASS].rearrange("(p j) n -> p j n", j=PACK))
+
+        def load_rows(vec, name):
+            col = keep.tile([P, R_PASSES, PACK], F32, name=name)
+            nc.sync.dma_start(out=col[:], in_=vec.rearrange("(a p t) -> p a t", p=P, t=PACK))
+            return col
+
+        nc.sync.dma_start(idx[:], offs)
+        for g in range(K_PASSES):
+            nc.sync.dma_start(out=tab[g][:].bitcast(I32), in_=tab_words[g].rearrange("p t i -> p (t i)").bitcast(I32))
+            if g == 0:
+                for q in range(QUADS):
+                    nc.sync.dma_start(
+                        out=tab_plane[32 * q : 32 * q + 4 * K_PASSES, :].bitcast(I32),
+                        in_=tab_scales[:, 4 * q : 4 * q + 4, :].bitcast(I32),
+                    )
+        load_w1(0, 0)
+        gain_c = load_rows(gain, "gain_c")
+        nc.sync.dma_start(p1[:], pos1)
+        load_w1(0, 1, parts=2)
+        nc.sync.dma_start(p2[:], pos2)
+        slope_c = load_rows(slope, "slope_c")
+        bend_c = load_rows(bend, "bend_c")
+        load_hip(0)
+        load_w1(1, 0)
+        load_w1(1, 1)
+        load_hip(1)
+        load_w1(2, 0)
+        load_w1(2, 1)
+        load_hip(2)
+        wsp_codes = keep.tile([P, R_PASSES, 2 * N], U8, name="wsp_codes", align_bytes=64)
+        nc.sync.dma_start(out=wsp_codes[:].bitcast(I32), in_=wsp_words.rearrange("a p c -> p a c").bitcast(I32))
+        for q in range(QUADS):
+            nc.sync.dma_start(
+                out=wsp_plane[32 * q : 32 * q + 4].bitcast(I32),
+                in_=wsp_scales[:, 4 * q : 4 * q + 4, :].rearrange("a r n -> r a n").bitcast(I32),
+            )
+        shift_c = keep.tile([P, N_TILES], F32, name="shift_c")
+        with nc.allow_non_contiguous_dma(reason="one value a partition"):
+            nc.sync.dma_start(out=shift_c[:], in_=shift.rearrange("(c p) -> p c", p=P))
+        for a in range(R_PASSES):
+            load_whip(a)
+
+        v_plane = keep.tile([P, S], U8, name="v_plane", align_bytes=64)
+        nc.vector.tensor_copy(v_plane[:], tab_plane[:].indirect(idx[:]))
+        v_codes = []
+        for g in range(K_PASSES):
+            picked = keep.tile([P, S], U32, name=f"v_codes{g}", align_bytes=64)
+            nc.vector.tensor_copy(picked[:], tab[g][:].indirect(idx[:]))
+            v_codes.append(picked)
+
+        def quantise(grouped, width, name, bufs, parts=1):
+            codes = ring.tile([P, width], U32, name=name + "_codes", tag=name + "_codes", bufs=bufs, align_bytes=64)
+            plane = ring.tile([P, width], U8, name=name + "_plane", tag=name + "_plane", bufs=bufs, align_bytes=64)
+            step = width // parts
+            for c in range(0, width, step):
+                nc.vector.quantize_mx(
+                    out=codes[:, c : c + step].bitcast(FP8X4),
+                    scales=plane[:, c : c + step],
+                    in_=grouped[:, PACK * c : PACK * (c + step)],
+                )
+            return codes, plane
+
+        w1_grouped = {}
+        w1_q = {}
+
+        def round_w1(a, g, engines):
+            grouped = ring.tile([P, PASS * PACK], BF16, name="w_grouped", tag="w_grouped", bufs=3, align_bytes=64)
+            dst = grouped[:].rearrange("p (t m j) -> p m j t", t=PACK, j=PACK)
+            rows = P // len(engines)
+            for u, eng in enumerate(engines):
+                src = w1_raw[(a, g)][:, u].rearrange("p j (m t) -> p m j t", t=PACK)
+                eng(dst[:, u * rows : (u + 1) * rows], src)
+            w1_grouped[(a, g)] = grouped
+
+        def quantise_w1(a, g, parts=1):
+            w1_q[(a, g)] = quantise(w1_grouped[(a, g)], PASS, "w1", 6, parts)
+
+        def weave(eng, grouped, planes):
+            eng(
+                grouped[:].rearrange("p (c i t) -> p c t i", i=4, t=PACK),
+                planes[:].rearrange("p t (c i) -> p c t i", i=4),
+            )
+
+        h = {}
+
+        def first_stage(a, t):
+            h[(a, t)] = ring.tile([P, S], F32, name="h", tag="h", bufs=6)
+            for half in range(S // BANK):
+                cols = slice(half * BANK, (half + 1) * BANK)
+                bank = psum.tile([P, BANK], F32, name="bank", tag="bank", bufs=5)
+                for g in range(K_PASSES):
+                    codes, plane = w1_q[(a, g)]
+                    nc.tensor.matmul_mx(
+                        out=bank[:],
+                        lhsT=codes[:, t * P : (t + 1) * P].bitcast(FP8X4),
+                        lhsT_scale=plane[:, t * P : (t + 1) * P],
+                        rhs=v_codes[g][:, cols].bitcast(FP8X4),
+                        rhs_scale=v_plane[4 * g : P, cols],
+                        start=(g == 0),
+                        stop=(g == K_PASSES - 1),
+                    )
+                nc.scalar.activation(h[(a, t)][:, cols], bank[:], ACT.Copy, scale=gain_c[:, a, t : t + 1])
+
+        sp = {}
+        th = {}
+        xa_planes = {}
+        xb_planes = {}
+
+        def pick(a, t):
+            if t == 0:
+                xb_planes[a] = ring.tile([P, PACK, PAIRS], F32, name="xb_planes", tag="xb_planes", bufs=2)
+            sp[(a, t)] = ring.tile([P, PAIRS], F32, name="sp", tag="sp", bufs=5)
+            nc.vector.tensor_copy(sp[(a, t)][:], h[(a, t)][:].indirect(p1[:]))
+            nc.vector.tensor_tensor(xb_planes[a][:, t, :], h[(a, t)][:].indirect(p2[:]), hip[a][:, t, :], MULT)
+
+        def bent(a, t):
+            th[(a, t)] = ring.tile([P, PAIRS], F32, name="th", tag="th", bufs=4)
+            nc.scalar.activation(th[(a, t)][:], sp[(a, t)][:], ACT.Tanh, scale=slope_c[:, a, t : t + 1])
+
+        def spine(a, t):
+            if t == 0:
+                xa_planes[a] = ring.tile([P, PACK, PAIRS], BF16, name="xa_planes", tag="xa_planes", bufs=2)
+            nc.vector.scalar_tensor_tensor(
+                xa_planes[a][:, t, :], th[(a, t)][:], bend_c[:, a, t : t + 1], sp[(a, t)][:], MULT, ADD
+            )
+
+        def woven(eng, planes):
+            grouped = ring.tile([P, PAIRS * PACK], BF16, name="x_grouped", tag="x_grouped", bufs=3, align_bytes=64)
+            weave(eng, grouped, planes)
+            return grouped
+
+        scores = [psum.tile([P, PAIRS], F32, name=f"scores{c}") for c in range(N_TILES)]
+
+        def second_stage(weights, x, first, last):
+            for c in range(N_TILES):
+                codes, plane = weights(c)
+                nc.tensor.matmul_mx(
+                    out=scores[c][:],
+                    lhsT=codes,
+                    lhsT_scale=plane,
+                    rhs=x[0][:].bitcast(FP8X4),
+                    rhs_scale=x[1][:],
+                    start=first,
+                    stop=last,
+                )
+
+        def wsp_of(a):
+            return lambda c: (
+                wsp_codes[:, a, 2 * P * c : 2 * P * (c + 1)].bitcast(FP4X4),
+                wsp_plane[:, a, P * c : P * (c + 1)],
+            )
+
+        whip_q = {}
+
+        def whip_of(a):
+            return lambda c: (
+                whip_q[a][0][:, P * c : P * (c + 1)].bitcast(FP8X4),
+                whip_q[a][1][:, P * c : P * (c + 1)],
+            )
+
+        def prepare_whip(a):
+            grouped = ring.tile([P, N * PACK], BF16, name="w_grouped", tag="w_grouped", bufs=3, align_bytes=64)
+            weave(nc.scalar.copy, grouped, whip_raw[a])
+            whip_q[a] = quantise(grouped, N, "whip", 3)
+
+        round_w1(0, 0, [nc.scalar.copy])
+        quantise_w1(0, 0)
+        round_w1(0, 1, [nc.scalar.copy, nc.vector.tensor_copy])
+        quantise_w1(0, 1, parts=2)
+
+        xb_q = {}
+        for a in range(R_PASSES):
+            last = a == R_PASSES - 1
+            for t in range(PACK):
+                first_stage(a, t)
+                pick(a, t)
+            if last:
+                for b in range(R_PASSES):
+                    prepare_whip(b)
+                    if b < a:
+                        second_stage(whip_of(b), xb_q[b], False, False)
+            for g in range(K_PASSES):
+                if not last:
+                    round_w1(a + 1, g, [nc.scalar.copy])
+                    quantise_w1(a + 1, g)
+                for t in (2 * g, 2 * g + 1):
+                    bent(a, t)
+                    spine(a, t)
+            xa_q = quantise(woven(nc.vector.tensor_copy, xa_planes[a]), PAIRS, "x", 2)
+            second_stage(wsp_of(a), xa_q, a == 0, False)
+            xb_q[a] = quantise(woven(nc.scalar.copy, xb_planes[a]), PAIRS, "xb", 3)
+        second_stage(whip_of(R_PASSES - 1), xb_q[R_PASSES - 1], False, True)
+
+        for c in range(N_TILES):
+            res = ring.tile([P, PAIRS], F32, name="res", tag="res", bufs=3)
+            if c == 1:
+                nc.vector.tensor_scalar_add(res[:], scores[c][:], shift_c[:, c : c + 1])
+            else:
+                nc.scalar.activation(res[:], scores[c][:], ACT.Identity, bias=shift_c[:, c : c + 1])
+            nc.sync.dma_start(out=out[c * P : (c + 1) * P, :], in_=res[:])

@@ -138,16 +138,17 @@ def tile_list_spine_hip_scores_kernel(
             rows = P // len(engines)
             for u, eng in enumerate(engines):
                 src = w1_raw[(a, g)][:, u].rearrange("p j (m t) -> p m j t", t=PACK)
-                eng(dst[:, u * rows : (u + 1) * rows], src)
+                for t in range(0, PACK, 2):
+                    eng(dst[:, u * rows : (u + 1) * rows, :, t : t + 2], src[:, :, :, t : t + 2])
             w1_grouped[(a, g)] = grouped
 
         def quantise_w1(a, g, parts=1):
             w1_q[(a, g)] = quantise(w1_grouped[(a, g)], PASS, "w1", 6, parts)
 
-        def weave(eng, grouped, planes):
+        def weave(eng, grouped, planes, run):
             eng(
-                grouped[:].rearrange("p (c i t) -> p c t i", i=4, t=PACK),
-                planes[:].rearrange("p t (c i) -> p c t i", i=4),
+                grouped[:].rearrange("p (c i t) -> p c t i", i=run, t=PACK),
+                planes[:].rearrange("p t (c i) -> p c t i", i=run),
             )
 
         h = {}
@@ -193,9 +194,9 @@ def tile_list_spine_hip_scores_kernel(
                 xa_planes[a][:, t, :], th[(a, t)][:], bend_c[:, a, t : t + 1], sp[(a, t)][:], MULT, ADD
             )
 
-        def woven(eng, planes):
+        def woven(eng, planes, run):
             grouped = ring.tile([P, PAIRS * PACK], BF16, name="x_grouped", tag="x_grouped", bufs=3, align_bytes=64)
-            weave(eng, grouped, planes)
+            weave(eng, grouped, planes, run)
             return grouped
 
         scores = [psum.tile([P, PAIRS], F32, name=f"scores{c}") for c in range(N_TILES)]
@@ -229,7 +230,7 @@ def tile_list_spine_hip_scores_kernel(
 
         def prepare_whip(a):
             grouped = ring.tile([P, N * PACK], BF16, name="w_grouped", tag="w_grouped", bufs=3, align_bytes=64)
-            weave(nc.scalar.copy, grouped, whip_raw[a])
+            weave(nc.scalar.copy, grouped, whip_raw[a], 2)
             whip_q[a] = quantise(grouped, N, "whip", 3)
 
         round_w1(0, 0, [nc.scalar.copy])
@@ -255,9 +256,9 @@ def tile_list_spine_hip_scores_kernel(
                 for t in (2 * g, 2 * g + 1):
                     bent(a, t)
                     spine(a, t)
-            xa_q = quantise(woven(nc.vector.tensor_copy, xa_planes[a]), PAIRS, "x", 2)
+            xa_q = quantise(woven(nc.vector.tensor_copy, xa_planes[a], 4), PAIRS, "x", 2)
             second_stage(wsp_of(a), xa_q, a == 0, False)
-            xb_q[a] = quantise(woven(nc.scalar.copy, xb_planes[a]), PAIRS, "xb", 3)
+            xb_q[a] = quantise(woven(nc.scalar.copy, xb_planes[a], 2), PAIRS, "xb", 3)
         second_stage(whip_of(R_PASSES - 1), xb_q[R_PASSES - 1], False, True)
 
         for c in range(N_TILES):

@@ -73,29 +73,27 @@ def tile_list_spine_hip_scores_kernel(
             nc.sync.dma_start(out=col[:], in_=vec.rearrange("(a p t) -> p a t", p=P, t=PACK))
             return col
 
-        nc.sync.dma_start(idx[:], offs)
-        for g in range(K_PASSES):
+        def load_table(g):
             nc.sync.dma_start(out=tab[g][:].bitcast(I32), in_=tab_words[g].rearrange("p t i -> p (t i)").bitcast(I32))
-            if g == 0:
-                for q in range(QUADS):
-                    nc.sync.dma_start(
-                        out=tab_plane[32 * q : 32 * q + 4 * K_PASSES, :].bitcast(I32),
-                        in_=tab_scales[:, 4 * q : 4 * q + 4, :].bitcast(I32),
-                    )
+
+        nc.sync.dma_start(idx[:], offs)
+        load_table(0)
+        for q in range(QUADS):
+            nc.sync.dma_start(
+                out=tab_plane[32 * q : 32 * q + 4 * K_PASSES, :].bitcast(I32),
+                in_=tab_scales[:, 4 * q : 4 * q + 4, :].bitcast(I32),
+            )
         load_w1(0, 0)
+        load_table(1)
+        load_w1(0, 1, parts=2)
         gain_c = load_rows(gain, "gain_c")
         nc.sync.dma_start(p1[:], pos1)
-        load_w1(0, 1, parts=2)
         nc.sync.dma_start(p2[:], pos2)
         slope_c = load_rows(slope, "slope_c")
         bend_c = load_rows(bend, "bend_c")
         load_hip(0)
         load_w1(1, 0)
         load_w1(1, 1)
-        load_hip(1)
-        load_w1(2, 0)
-        load_w1(2, 1)
-        load_hip(2)
         wsp_codes = keep.tile([P, R_PASSES, 2 * N], U8, name="wsp_codes", align_bytes=64)
         nc.sync.dma_start(out=wsp_codes[:].bitcast(I32), in_=wsp_words.rearrange("a p c -> p a c").bitcast(I32))
         for q in range(QUADS):
@@ -103,11 +101,16 @@ def tile_list_spine_hip_scores_kernel(
                 out=wsp_plane[32 * q : 32 * q + 4].bitcast(I32),
                 in_=wsp_scales[:, 4 * q : 4 * q + 4, :].rearrange("a r n -> r a n").bitcast(I32),
             )
+        load_hip(1)
+        load_w1(2, 0)
+        load_w1(2, 1)
+        load_whip(0)
+        load_hip(2)
+        load_whip(1)
+        load_whip(2)
         shift_c = keep.tile([P, N_TILES], F32, name="shift_c")
         with nc.allow_non_contiguous_dma(reason="one value a partition"):
             nc.sync.dma_start(out=shift_c[:], in_=shift.rearrange("(c p) -> p c", p=P))
-        for a in range(R_PASSES):
-            load_whip(a)
 
         v_plane = keep.tile([P, S], U8, name="v_plane", align_bytes=64)
         nc.vector.tensor_copy(v_plane[:], tab_plane[:].indirect(idx[:]))
@@ -117,39 +120,35 @@ def tile_list_spine_hip_scores_kernel(
             nc.vector.tensor_copy(picked[:], tab[g][:].indirect(idx[:]))
             v_codes.append(picked)
 
-        def quantise(grouped, width, name, bufs, parts=1):
+        def mx_tiles(width, name, bufs):
             codes = ring.tile([P, width], U32, name=name + "_codes", tag=name + "_codes", bufs=bufs, align_bytes=64)
             plane = ring.tile([P, width], U8, name=name + "_plane", tag=name + "_plane", bufs=bufs, align_bytes=64)
-            step = width // parts
-            for c in range(0, width, step):
-                nc.vector.quantize_mx(
-                    out=codes[:, c : c + step].bitcast(FP8X4),
-                    scales=plane[:, c : c + step],
-                    in_=grouped[:, PACK * c : PACK * (c + step)],
-                )
             return codes, plane
 
-        w1_grouped = {}
+        def quantise(mx, grouped, c0, c1):
+            nc.vector.quantize_mx(
+                out=mx[0][:, c0:c1].bitcast(FP8X4), scales=mx[1][:, c0:c1], in_=grouped[:, PACK * c0 : PACK * c1]
+            )
+
         w1_q = {}
 
-        def round_w1(a, g, engines):
+        def prepare_w1(a, g, engines, parts):
             grouped = ring.tile([P, PASS * PACK], BF16, name="w_grouped", tag="w_grouped", bufs=3, align_bytes=64)
             dst = grouped[:].rearrange("p (t m j) -> p m j t", t=PACK, j=PACK)
             rows = P // len(engines)
-            for u, eng in enumerate(engines):
+            for u, pair in enumerate(engines):
                 src = w1_raw[(a, g)][:, u].rearrange("p j (m t) -> p m j t", t=PACK)
-                for t in range(0, PACK, 2):
+                for t, eng in zip((0, 2), pair):
                     eng(dst[:, u * rows : (u + 1) * rows, :, t : t + 2], src[:, :, :, t : t + 2])
-            w1_grouped[(a, g)] = grouped
+            w1_q[(a, g)] = mx_tiles(PASS, "w1", 6)
+            for c0 in range(0, PASS, PASS // parts):
+                quantise(w1_q[(a, g)], grouped, c0, c0 + PASS // parts)
 
-        def quantise_w1(a, g, parts=1):
-            w1_q[(a, g)] = quantise(w1_grouped[(a, g)], PASS, "w1", 6, parts)
+        def woven(grouped, run, c0, c1):
+            return grouped[:, PACK * c0 : PACK * c1].rearrange("p (c i t) -> p c t i", i=run, t=PACK)
 
-        def weave(eng, grouped, planes, run):
-            eng(
-                grouped[:].rearrange("p (c i t) -> p c t i", i=run, t=PACK),
-                planes[:].rearrange("p t (c i) -> p c t i", i=run),
-            )
+        def runs(planes, run, c0, c1):
+            return planes[:, :, c0:c1].rearrange("p t (c i) -> p c t i", i=run)
 
         h = {}
 
@@ -169,18 +168,23 @@ def tile_list_spine_hip_scores_kernel(
                         start=(g == 0),
                         stop=(g == K_PASSES - 1),
                     )
-                nc.scalar.activation(h[(a, t)][:, cols], bank[:], ACT.Copy, scale=gain_c[:, a, t : t + 1])
+                if (a, t, half) == (0, 0, 1):
+                    nc.vector.tensor_scalar_mul(h[(a, t)][:, cols], bank[:], gain_c[:, a, t : t + 1])
+                else:
+                    nc.scalar.activation(h[(a, t)][:, cols], bank[:], ACT.Copy, scale=gain_c[:, a, t : t + 1])
 
         sp = {}
         th = {}
         xa_planes = {}
         xb_planes = {}
 
-        def pick(a, t):
-            if t == 0:
-                xb_planes[a] = ring.tile([P, PACK, PAIRS], F32, name="xb_planes", tag="xb_planes", bufs=2)
+        def pick_spine(a, t):
             sp[(a, t)] = ring.tile([P, PAIRS], F32, name="sp", tag="sp", bufs=5)
             nc.vector.tensor_copy(sp[(a, t)][:], h[(a, t)][:].indirect(p1[:]))
+
+        def pick_hip(a, t):
+            if t == 0:
+                xb_planes[a] = ring.tile([P, PACK, PAIRS], F32, name="xb_planes", tag="xb_planes", bufs=2)
             nc.vector.tensor_tensor(xb_planes[a][:, t, :], h[(a, t)][:].indirect(p2[:]), hip[a][:, t, :], MULT)
 
         def bent(a, t):
@@ -194,77 +198,111 @@ def tile_list_spine_hip_scores_kernel(
                 xa_planes[a][:, t, :], th[(a, t)][:], bend_c[:, a, t : t + 1], sp[(a, t)][:], MULT, ADD
             )
 
-        def woven(eng, planes, run):
-            grouped = ring.tile([P, PAIRS * PACK], BF16, name="x_grouped", tag="x_grouped", bufs=3, align_bytes=64)
-            weave(eng, grouped, planes, run)
-            return grouped
+        xa_grouped = {}
+        xb_grouped = {}
+        xa_q = {}
+        xb_q = {}
 
-        scores = [psum.tile([P, PAIRS], F32, name=f"scores{c}") for c in range(N_TILES)]
+        def grouped_tile():
+            return ring.tile([P, PAIRS * PACK], BF16, name="x_grouped", tag="x_grouped", bufs=3, align_bytes=64)
 
-        def second_stage(weights, x, first, last):
-            for c in range(N_TILES):
-                codes, plane = weights(c)
-                nc.tensor.matmul_mx(
-                    out=scores[c][:],
-                    lhsT=codes,
-                    lhsT_scale=plane,
-                    rhs=x[0][:].bitcast(FP8X4),
-                    rhs_scale=x[1][:],
-                    start=first,
-                    stop=last,
-                )
+        def weave_xa(a, c0, c1, copy):
+            if c0 == 0:
+                xa_grouped[a] = grouped_tile()
+                xa_q[a] = mx_tiles(PAIRS, "xa", 3)
+            copy(woven(xa_grouped[a], 4, c0, c1), runs(xa_planes[a], 4, c0, c1))
 
-        def wsp_of(a):
-            return lambda c: (
-                wsp_codes[:, a, 2 * P * c : 2 * P * (c + 1)].bitcast(FP4X4),
-                wsp_plane[:, a, P * c : P * (c + 1)],
-            )
+        def weave_xb(a, c0, c1):
+            if c0 == 0:
+                xb_grouped[a] = grouped_tile()
+                xb_q[a] = mx_tiles(PAIRS, "xb", 3)
+            nc.scalar.copy(woven(xb_grouped[a], 2, c0, c1), runs(xb_planes[a], 2, c0, c1))
 
         whip_q = {}
 
-        def whip_of(a):
-            return lambda c: (
-                whip_q[a][0][:, P * c : P * (c + 1)].bitcast(FP8X4),
-                whip_q[a][1][:, P * c : P * (c + 1)],
-            )
-
         def prepare_whip(a):
             grouped = ring.tile([P, N * PACK], BF16, name="w_grouped", tag="w_grouped", bufs=3, align_bytes=64)
-            weave(nc.scalar.copy, grouped, whip_raw[a], 2)
-            whip_q[a] = quantise(grouped, N, "whip", 3)
+            nc.scalar.copy(woven(grouped, 2, 0, N), runs(whip_raw[a], 2, 0, N))
+            whip_q[a] = mx_tiles(N, "whip", 3)
+            quantise(whip_q[a], grouped, 0, N)
 
-        round_w1(0, 0, [nc.scalar.copy])
-        quantise_w1(0, 0)
-        round_w1(0, 1, [nc.scalar.copy, nc.vector.tensor_copy])
-        quantise_w1(0, 1, parts=2)
+        HALF = PAIRS // 2
+        scores = {(0, c): psum.tile([P, HALF], F32, name=f"scores{c}") for c in range(N_TILES)}
 
-        xb_q = {}
+        def score_pass(u, c, codes, plane, x, first, last):
+            cols = slice(u * HALF, (u + 1) * HALF)
+            nc.tensor.matmul_mx(
+                out=scores[(u, c)][:],
+                lhsT=codes,
+                lhsT_scale=plane,
+                rhs=x[0][:, cols].bitcast(FP8X4),
+                rhs_scale=x[1][:, cols],
+                start=first,
+                stop=last,
+            )
+
+        def spine_scores(a, u):
+            for c in range(N_TILES):
+                codes = wsp_codes[:, a, 2 * P * c : 2 * P * (c + 1)].bitcast(FP4X4)
+                score_pass(u, c, codes, wsp_plane[:, a, P * c : P * (c + 1)], xa_q[a], a == 0, a == R_PASSES - 1)
+
+        def hip_scores(a, u):
+            for c in range(N_TILES):
+                codes = whip_q[a][0][:, P * c : P * (c + 1)].bitcast(FP8X4)
+                score_pass(u, c, codes, whip_q[a][1][:, P * c : P * (c + 1)], xb_q[a], False, False)
+
+        def store(u, on_vector):
+            for c in range(N_TILES):
+                res = ring.tile([P, HALF], F32, name="res", tag="res", bufs=2 * N_TILES)
+                if c in on_vector:
+                    nc.vector.tensor_scalar_add(res[:], scores[(u, c)][:], shift_c[:, c : c + 1])
+                else:
+                    nc.scalar.activation(res[:], scores[(u, c)][:], ACT.Identity, bias=shift_c[:, c : c + 1])
+                nc.sync.dma_start(out=out[c * P : (c + 1) * P, u * HALF : (u + 1) * HALF], in_=res[:])
+
+        on_scalar = [(nc.scalar.copy, nc.scalar.copy)]
+        prepare_w1(0, 0, on_scalar, 1)
+        prepare_w1(0, 1, on_scalar + [(nc.vector.tensor_copy, nc.scalar.copy)], 2)
+
+        last = R_PASSES - 1
         for a in range(R_PASSES):
-            last = a == R_PASSES - 1
             for t in range(PACK):
                 first_stage(a, t)
-                pick(a, t)
-            if last:
-                for b in range(R_PASSES):
-                    prepare_whip(b)
-                    if b < a:
-                        second_stage(whip_of(b), xb_q[b], False, False)
-            for g in range(K_PASSES):
-                if not last:
-                    round_w1(a + 1, g, [nc.scalar.copy])
-                    quantise_w1(a + 1, g)
-                for t in (2 * g, 2 * g + 1):
-                    bent(a, t)
-                    spine(a, t)
-            xa_q = quantise(woven(nc.vector.tensor_copy, xa_planes[a], 4), PAIRS, "x", 2)
-            second_stage(wsp_of(a), xa_q, a == 0, False)
-            xb_q[a] = quantise(woven(nc.scalar.copy, xb_planes[a], 2), PAIRS, "xb", 3)
-        second_stage(whip_of(R_PASSES - 1), xb_q[R_PASSES - 1], False, True)
+                pick_spine(a, t)
+                if t >= 1:
+                    bent(a, t - 1)
+                pick_hip(a, t)
+                if a < last and t in (1, 2):
+                    prepare_w1(a + 1, t - 1, on_scalar, 1)
+                if a == last and t < R_PASSES:
+                    prepare_whip(t)
+                if t >= 1:
+                    spine(a, t - 1)
+                if a > 0 and t == 0:
+                    weave_xa(a - 1, 0, HALF, nc.scalar.copy)
+                    weave_xa(a - 1, HALF, PAIRS, nc.vector.tensor_copy)
+                    quantise(xa_q[a - 1], xa_grouped[a - 1], 0, PAIRS)
+                    spine_scores(a - 1, 0)
+                if a > 0 and t == PACK - 1:
+                    weave_xb(a - 1, 0, PAIRS)
+                    quantise(xb_q[a - 1], xb_grouped[a - 1], 0, PAIRS)
+            bent(a, PACK - 1)
+            spine(a, PACK - 1)
 
         for c in range(N_TILES):
-            res = ring.tile([P, PAIRS], F32, name="res", tag="res", bufs=3)
-            if c == 1:
-                nc.vector.tensor_scalar_add(res[:], scores[c][:], shift_c[:, c : c + 1])
-            else:
-                nc.scalar.activation(res[:], scores[c][:], ACT.Identity, bias=shift_c[:, c : c + 1])
-            nc.sync.dma_start(out=out[c * P : (c + 1) * P, :], in_=res[:])
+            scores[(1, c)] = psum.tile([P, HALF], F32, name="bank", tag="bank", bufs=5)
+        for a in range(last):
+            hip_scores(a, 0)
+        for a in range(last):
+            spine_scores(a, 1)
+            hip_scores(a, 1)
+        for u in range(2):
+            weave_xb(last, u * HALF, (u + 1) * HALF)
+        for u in range(2):
+            weave_xa(last, u * HALF, (u + 1) * HALF, nc.vector.tensor_copy)
+            quantise(xb_q[last], xb_grouped[last], u * HALF, (u + 1) * HALF)
+            hip_scores(last, u)
+            quantise(xa_q[last], xa_grouped[last], u * HALF, (u + 1) * HALF)
+            spine_scores(last, u)
+        store(0, ())
+        store(1, (0, 2))

@@ -1,6 +1,7 @@
 from contextlib import ExitStack
 
 import concourse.mybir as mybir
+from concourse.masks import make_identity
 
 K, T, S, PAIRS, H, N = 1024, 4096, 1024, 512, 1536, 384
 FLOPS = 2 * K * H * S + 2 * 2 * H * N * PAIRS
@@ -23,8 +24,27 @@ PASS = P * PACK
 BANK = 512
 K_PASSES = K // PASS
 R_PASSES = H // PASS
+LAST = R_PASSES - 1
 N_TILES = N // P
+HALF = PAIRS // 2
+LIST_GROUP = 16
 QUADS = 4
+QUAD = P // QUADS
+SCALE_ROWS = 4
+GAIN, SLOPE, BEND = 0, 1, 2
+FACTOR_ROWS = 3 * R_PASSES
+
+RUN_F32, RUN_BF16 = 2, 4
+
+RAW_BUFS = 4
+W_GROUPED_BUFS = 3
+W1_MX_BUFS = 2 * K_PASSES
+H_BUFS = PACK + 2
+STAGE_BANKS = 5
+SP_BUFS = PACK + 1
+TH_BUFS = PACK
+PLANE_BUFS = 2
+X_GROUPED_BUFS = 3
 
 
 def tile_list_spine_hip_scores_kernel(
@@ -41,9 +61,9 @@ def tile_list_spine_hip_scores_kernel(
         nc.vector.memset(tab_plane[:].bitcast(I32), 0)
         nc.vector.memset(wsp_plane[:].rearrange("p a n -> p (a n)").bitcast(I32), 0)
 
-        idx = keep.tile([P, S // 16], U16, name="idx")
-        p1 = keep.tile([P, PAIRS // 16], U16, name="p1")
-        p2 = keep.tile([P, PAIRS // 16], U16, name="p2")
+        idx = keep.tile([P, S // LIST_GROUP], U16, name="idx")
+        p1 = keep.tile([P, PAIRS // LIST_GROUP], U16, name="p1")
+        p2 = keep.tile([P, PAIRS // LIST_GROUP], U16, name="p2")
         tab = [keep.tile([P, T], U32, name=f"tab{g}") for g in range(K_PASSES)]
         w1_raw = {}
         hip = {}
@@ -51,12 +71,12 @@ def tile_list_spine_hip_scores_kernel(
 
         def load_w1(a, g, parts=1):
             width = PASS // parts
-            raw = ring.tile([P, parts, PACK, width], F32, name="raw", tag="raw", bufs=4)
+            raw = ring.tile([P, parts, PACK, width], F32, name="raw", tag="raw", bufs=RAW_BUFS)
             w1_raw[(a, g)] = raw
-            for u in range(parts):
-                c0 = a * PASS + u * width
+            for part in range(parts):
+                c0 = a * PASS + part * width
                 nc.sync.dma_start(
-                    out=raw[:, u],
+                    out=raw[:, part],
                     in_=w1[g * PASS : (g + 1) * PASS, c0 : c0 + width].rearrange("(p j) c -> p j c", j=PACK),
                 )
 
@@ -65,13 +85,13 @@ def tile_list_spine_hip_scores_kernel(
             nc.sync.dma_start(out=hip[a][:], in_=hipm[a * PASS : (a + 1) * PASS].rearrange("(p t) j -> p t j", t=PACK))
 
         def load_whip(a):
-            whip_raw[a] = ring.tile([P, PACK, N], F32, name="raw", tag="raw", bufs=4)
-            nc.sync.dma_start(out=whip_raw[a][:], in_=whip[a * PASS : (a + 1) * PASS].rearrange("(p j) n -> p j n", j=PACK))
+            whip_raw[a] = ring.tile([P, PACK, N], F32, name="raw", tag="raw", bufs=RAW_BUFS)
+            nc.sync.dma_start(out=whip_raw[a][:], in_=whip[a * PASS : (a + 1) * PASS].rearrange("(p t) n -> p t n", t=PACK))
 
-        def load_rows(vec, name):
-            col = keep.tile([P, R_PASSES, PACK], F32, name=name)
-            nc.sync.dma_start(out=col[:], in_=vec.rearrange("(a p t) -> p a t", p=P, t=PACK))
-            return col
+        factor_rows = keep.tile([P, PASS], F32, name="factor_rows")
+        nc.gpsimd.memset(factor_rows[:], 0.0)
+        identity = keep.tile([P, P], F32, name="identity")
+        make_identity(nc, identity[:])
 
         def load_table(g):
             nc.sync.dma_start(out=tab[g][:].bitcast(I32), in_=tab_words[g].rearrange("p t i -> p (t i)").bitcast(I32))
@@ -80,17 +100,19 @@ def tile_list_spine_hip_scores_kernel(
         load_table(0)
         for q in range(QUADS):
             nc.sync.dma_start(
-                out=tab_plane[32 * q : 32 * q + 4 * K_PASSES, :].bitcast(I32),
-                in_=tab_scales[:, 4 * q : 4 * q + 4, :].bitcast(I32),
+                out=tab_plane[QUAD * q : QUAD * q + SCALE_ROWS * K_PASSES, :].bitcast(I32),
+                in_=tab_scales[:, SCALE_ROWS * q : SCALE_ROWS * (q + 1), :].bitcast(I32),
             )
         load_w1(0, 0)
         load_table(1)
+        for i, vec in enumerate((gain, slope, bend)):
+            nc.sync.dma_start(
+                out=factor_rows[R_PASSES * i : R_PASSES * (i + 1), :], in_=vec.rearrange("(a c) -> a c", c=PASS)
+            )
+        nc.sync.dma_start(out=factor_rows[FACTOR_ROWS : FACTOR_ROWS + N_TILES, :P], in_=shift.rearrange("(c p) -> c p", p=P))
         load_w1(0, 1, parts=2)
-        gain_c = load_rows(gain, "gain_c")
         nc.sync.dma_start(p1[:], pos1)
         nc.sync.dma_start(p2[:], pos2)
-        slope_c = load_rows(slope, "slope_c")
-        bend_c = load_rows(bend, "bend_c")
         load_hip(0)
         load_w1(1, 0)
         load_w1(1, 1)
@@ -98,8 +120,8 @@ def tile_list_spine_hip_scores_kernel(
         nc.sync.dma_start(out=wsp_codes[:].bitcast(I32), in_=wsp_words.rearrange("a p c -> p a c").bitcast(I32))
         for q in range(QUADS):
             nc.sync.dma_start(
-                out=wsp_plane[32 * q : 32 * q + 4].bitcast(I32),
-                in_=wsp_scales[:, 4 * q : 4 * q + 4, :].rearrange("a r n -> r a n").bitcast(I32),
+                out=wsp_plane[QUAD * q : QUAD * q + SCALE_ROWS].bitcast(I32),
+                in_=wsp_scales[:, SCALE_ROWS * q : SCALE_ROWS * (q + 1), :].rearrange("a r n -> r a n").bitcast(I32),
             )
         load_hip(1)
         load_w1(2, 0)
@@ -108,9 +130,6 @@ def tile_list_spine_hip_scores_kernel(
         load_hip(2)
         load_whip(1)
         load_whip(2)
-        shift_c = keep.tile([P, N_TILES], F32, name="shift_c")
-        with nc.allow_non_contiguous_dma(reason="one value a partition"):
-            nc.sync.dma_start(out=shift_c[:], in_=shift.rearrange("(c p) -> p c", p=P))
 
         v_plane = keep.tile([P, S], U8, name="v_plane", align_bytes=64)
         nc.vector.tensor_copy(v_plane[:], tab_plane[:].indirect(idx[:]))
@@ -119,6 +138,20 @@ def tile_list_spine_hip_scores_kernel(
             picked = keep.tile([P, S], U32, name=f"v_codes{g}", align_bytes=64)
             nc.vector.tensor_copy(picked[:], tab[g][:].indirect(idx[:]))
             v_codes.append(picked)
+
+        turned = psum.tile([P, PACK, P], F32, name="turned", tag="scores0")
+        for t in range(PACK):
+            nc.tensor.transpose(turned[:, t, :], factor_rows[:, t:PASS:PACK], identity[:])
+        factors = keep.tile([P, PACK, FACTOR_ROWS], F32, name="factors")
+        nc.scalar.copy(factors[:], turned[:, :, :FACTOR_ROWS])
+
+        turned_shift = psum.tile([P, P], F32, name="turned_shift", tag="scores1")
+        nc.tensor.transpose(turned_shift[:], factor_rows[:, :P], identity[:])
+        shift_c = keep.tile([P, N_TILES], F32, name="shift_c")
+        nc.scalar.copy(shift_c[:], turned_shift[:, FACTOR_ROWS : FACTOR_ROWS + N_TILES])
+
+        def factor(i, a, t):
+            return factors[:, t, R_PASSES * i + a : R_PASSES * i + a + 1]
 
         def mx_tiles(width, name, bufs):
             codes = ring.tile([P, width], U32, name=name + "_codes", tag=name + "_codes", bufs=bufs, align_bytes=64)
@@ -132,31 +165,31 @@ def tile_list_spine_hip_scores_kernel(
 
         w1_q = {}
 
-        def prepare_w1(a, g, engines, parts):
-            grouped = ring.tile([P, PASS * PACK], BF16, name="w_grouped", tag="w_grouped", bufs=3, align_bytes=64)
+        def prepare_w1(a, g, copies, calls):
+            grouped = ring.tile([P, PASS * PACK], BF16, name="w_grouped", tag="w_grouped", bufs=W_GROUPED_BUFS, align_bytes=64)
             dst = grouped[:].rearrange("p (t m j) -> p m j t", t=PACK, j=PACK)
-            rows = P // len(engines)
-            for u, pair in enumerate(engines):
-                src = w1_raw[(a, g)][:, u].rearrange("p j (m t) -> p m j t", t=PACK)
-                for t, eng in zip((0, 2), pair):
-                    eng(dst[:, u * rows : (u + 1) * rows, :, t : t + 2], src[:, :, :, t : t + 2])
-            w1_q[(a, g)] = mx_tiles(PASS, "w1", 6)
-            for c0 in range(0, PASS, PASS // parts):
-                quantise(w1_q[(a, g)], grouped, c0, c0 + PASS // parts)
+            m_width = P // len(copies)
+            for part, pair in enumerate(copies):
+                src = w1_raw[(a, g)][:, part].rearrange("p j (m t) -> p m j t", t=PACK)
+                for t, copy in zip((0, 2), pair):
+                    copy(dst[:, part * m_width : (part + 1) * m_width, :, t : t + 2], src[:, :, :, t : t + 2])
+            w1_q[(a, g)] = mx_tiles(PASS, "w1", W1_MX_BUFS)
+            for c0 in range(0, PASS, PASS // calls):
+                quantise(w1_q[(a, g)], grouped, c0, c0 + PASS // calls)
 
         def woven(grouped, run, c0, c1):
             return grouped[:, PACK * c0 : PACK * c1].rearrange("p (c i t) -> p c t i", i=run, t=PACK)
 
-        def runs(planes, run, c0, c1):
-            return planes[:, :, c0:c1].rearrange("p t (c i) -> p c t i", i=run)
+        def runs(by_t, run, c0, c1):
+            return by_t[:, :, c0:c1].rearrange("p t (c i) -> p c t i", i=run)
 
         h = {}
 
         def first_stage(a, t):
-            h[(a, t)] = ring.tile([P, S], F32, name="h", tag="h", bufs=6)
-            for half in range(S // BANK):
-                cols = slice(half * BANK, (half + 1) * BANK)
-                bank = psum.tile([P, BANK], F32, name="bank", tag="bank", bufs=5)
+            h[(a, t)] = ring.tile([P, S], F32, name="h", tag="h", bufs=H_BUFS)
+            for b in range(S // BANK):
+                cols = slice(b * BANK, (b + 1) * BANK)
+                bank = psum.tile([P, BANK], F32, name="bank", tag="bank", bufs=STAGE_BANKS)
                 for g in range(K_PASSES):
                     codes, plane = w1_q[(a, g)]
                     nc.tensor.matmul_mx(
@@ -164,38 +197,38 @@ def tile_list_spine_hip_scores_kernel(
                         lhsT=codes[:, t * P : (t + 1) * P].bitcast(FP8X4),
                         lhsT_scale=plane[:, t * P : (t + 1) * P],
                         rhs=v_codes[g][:, cols].bitcast(FP8X4),
-                        rhs_scale=v_plane[4 * g : P, cols],
+                        rhs_scale=v_plane[SCALE_ROWS * g : P, cols],
                         start=(g == 0),
                         stop=(g == K_PASSES - 1),
                     )
-                if (a, t, half) == (0, 0, 1):
-                    nc.vector.tensor_scalar_mul(h[(a, t)][:, cols], bank[:], gain_c[:, a, t : t + 1])
+                if a == 0 and t == 0 and b == 1:
+                    nc.vector.tensor_scalar_mul(h[(a, t)][:, cols], bank[:], factor(GAIN, a, t))
                 else:
-                    nc.scalar.activation(h[(a, t)][:, cols], bank[:], ACT.Copy, scale=gain_c[:, a, t : t + 1])
+                    nc.scalar.activation(h[(a, t)][:, cols], bank[:], ACT.Copy, scale=factor(GAIN, a, t))
 
         sp = {}
         th = {}
-        xa_planes = {}
-        xb_planes = {}
+        xa_by_t = {}
+        xb_by_t = {}
 
         def pick_spine(a, t):
-            sp[(a, t)] = ring.tile([P, PAIRS], F32, name="sp", tag="sp", bufs=5)
+            sp[(a, t)] = ring.tile([P, PAIRS], F32, name="sp", tag="sp", bufs=SP_BUFS)
             nc.vector.tensor_copy(sp[(a, t)][:], h[(a, t)][:].indirect(p1[:]))
 
         def pick_hip(a, t):
             if t == 0:
-                xb_planes[a] = ring.tile([P, PACK, PAIRS], F32, name="xb_planes", tag="xb_planes", bufs=2)
-            nc.vector.tensor_tensor(xb_planes[a][:, t, :], h[(a, t)][:].indirect(p2[:]), hip[a][:, t, :], MULT)
+                xb_by_t[a] = ring.tile([P, PACK, PAIRS], F32, name="xb_by_t", tag="xb_by_t", bufs=PLANE_BUFS)
+            nc.vector.tensor_tensor(xb_by_t[a][:, t, :], h[(a, t)][:].indirect(p2[:]), hip[a][:, t, :], MULT)
 
         def bent(a, t):
-            th[(a, t)] = ring.tile([P, PAIRS], F32, name="th", tag="th", bufs=4)
-            nc.scalar.activation(th[(a, t)][:], sp[(a, t)][:], ACT.Tanh, scale=slope_c[:, a, t : t + 1])
+            th[(a, t)] = ring.tile([P, PAIRS], F32, name="th", tag="th", bufs=TH_BUFS)
+            nc.scalar.activation(th[(a, t)][:], sp[(a, t)][:], ACT.Tanh, scale=factor(SLOPE, a, t))
 
         def spine(a, t):
             if t == 0:
-                xa_planes[a] = ring.tile([P, PACK, PAIRS], BF16, name="xa_planes", tag="xa_planes", bufs=2)
+                xa_by_t[a] = ring.tile([P, PACK, PAIRS], BF16, name="xa_by_t", tag="xa_by_t", bufs=PLANE_BUFS)
             nc.vector.scalar_tensor_tensor(
-                xa_planes[a][:, t, :], th[(a, t)][:], bend_c[:, a, t : t + 1], sp[(a, t)][:], MULT, ADD
+                xa_by_t[a][:, t, :], th[(a, t)][:], factor(BEND, a, t), sp[(a, t)][:], MULT, ADD
             )
 
         xa_grouped = {}
@@ -204,32 +237,31 @@ def tile_list_spine_hip_scores_kernel(
         xb_q = {}
 
         def grouped_tile():
-            return ring.tile([P, PAIRS * PACK], BF16, name="x_grouped", tag="x_grouped", bufs=3, align_bytes=64)
+            return ring.tile([P, PAIRS * PACK], BF16, name="x_grouped", tag="x_grouped", bufs=X_GROUPED_BUFS, align_bytes=64)
 
         def weave_xa(a, c0, c1, copy):
             if c0 == 0:
                 xa_grouped[a] = grouped_tile()
-                xa_q[a] = mx_tiles(PAIRS, "xa", 3)
-            copy(woven(xa_grouped[a], 4, c0, c1), runs(xa_planes[a], 4, c0, c1))
+                xa_q[a] = mx_tiles(PAIRS, "xa", R_PASSES)
+            copy(woven(xa_grouped[a], RUN_BF16, c0, c1), runs(xa_by_t[a], RUN_BF16, c0, c1))
 
         def weave_xb(a, c0, c1):
             if c0 == 0:
                 xb_grouped[a] = grouped_tile()
-                xb_q[a] = mx_tiles(PAIRS, "xb", 3)
-            nc.scalar.copy(woven(xb_grouped[a], 2, c0, c1), runs(xb_planes[a], 2, c0, c1))
+                xb_q[a] = mx_tiles(PAIRS, "xb", R_PASSES)
+            nc.scalar.copy(woven(xb_grouped[a], RUN_F32, c0, c1), runs(xb_by_t[a], RUN_F32, c0, c1))
 
         whip_q = {}
 
         def prepare_whip(a):
-            grouped = ring.tile([P, N * PACK], BF16, name="w_grouped", tag="w_grouped", bufs=3, align_bytes=64)
-            nc.scalar.copy(woven(grouped, 2, 0, N), runs(whip_raw[a], 2, 0, N))
-            whip_q[a] = mx_tiles(N, "whip", 3)
+            grouped = ring.tile([P, N * PACK], BF16, name="w_grouped", tag="w_grouped", bufs=W_GROUPED_BUFS, align_bytes=64)
+            nc.scalar.copy(woven(grouped, RUN_F32, 0, N), runs(whip_raw[a], RUN_F32, 0, N))
+            whip_q[a] = mx_tiles(N, "whip", R_PASSES)
             quantise(whip_q[a], grouped, 0, N)
 
-        HALF = PAIRS // 2
-        scores = {(0, c): psum.tile([P, HALF], F32, name=f"scores{c}") for c in range(N_TILES)}
+        scores = {(0, c): psum.tile([P, HALF], F32, name=f"scores{c}", tag=f"scores{c}") for c in range(N_TILES)}
 
-        def score_pass(u, c, codes, plane, x, first, last):
+        def score_pass(u, c, codes, plane, x, start, stop):
             cols = slice(u * HALF, (u + 1) * HALF)
             nc.tensor.matmul_mx(
                 out=scores[(u, c)][:],
@@ -237,14 +269,14 @@ def tile_list_spine_hip_scores_kernel(
                 lhsT_scale=plane,
                 rhs=x[0][:, cols].bitcast(FP8X4),
                 rhs_scale=x[1][:, cols],
-                start=first,
-                stop=last,
+                start=start,
+                stop=stop,
             )
 
         def spine_scores(a, u):
             for c in range(N_TILES):
                 codes = wsp_codes[:, a, 2 * P * c : 2 * P * (c + 1)].bitcast(FP4X4)
-                score_pass(u, c, codes, wsp_plane[:, a, P * c : P * (c + 1)], xa_q[a], a == 0, a == R_PASSES - 1)
+                score_pass(u, c, codes, wsp_plane[:, a, P * c : P * (c + 1)], xa_q[a], a == 0, a == LAST)
 
         def hip_scores(a, u):
             for c in range(N_TILES):
@@ -264,7 +296,6 @@ def tile_list_spine_hip_scores_kernel(
         prepare_w1(0, 0, on_scalar, 1)
         prepare_w1(0, 1, on_scalar + [(nc.vector.tensor_copy, nc.scalar.copy)], 2)
 
-        last = R_PASSES - 1
         for a in range(R_PASSES):
             for t in range(PACK):
                 first_stage(a, t)
@@ -272,9 +303,9 @@ def tile_list_spine_hip_scores_kernel(
                 if t >= 1:
                     bent(a, t - 1)
                 pick_hip(a, t)
-                if a < last and t in (1, 2):
+                if a < LAST and 1 <= t <= K_PASSES:
                     prepare_w1(a + 1, t - 1, on_scalar, 1)
-                if a == last and t < R_PASSES:
+                if a == LAST and t < R_PASSES:
                     prepare_whip(t)
                 if t >= 1:
                     spine(a, t - 1)
@@ -290,19 +321,20 @@ def tile_list_spine_hip_scores_kernel(
             spine(a, PACK - 1)
 
         for c in range(N_TILES):
-            scores[(1, c)] = psum.tile([P, HALF], F32, name="bank", tag="bank", bufs=5)
-        for a in range(last):
+            scores[(1, c)] = psum.tile([P, HALF], F32, name="bank", tag="bank", bufs=STAGE_BANKS)
+        for a in range(LAST):
             hip_scores(a, 0)
-        for a in range(last):
+        for a in range(LAST):
             spine_scores(a, 1)
             hip_scores(a, 1)
+
         for u in range(2):
-            weave_xb(last, u * HALF, (u + 1) * HALF)
+            weave_xb(LAST, u * HALF, (u + 1) * HALF)
         for u in range(2):
-            weave_xa(last, u * HALF, (u + 1) * HALF, nc.vector.tensor_copy)
-            quantise(xb_q[last], xb_grouped[last], u * HALF, (u + 1) * HALF)
-            hip_scores(last, u)
-            quantise(xa_q[last], xa_grouped[last], u * HALF, (u + 1) * HALF)
-            spine_scores(last, u)
+            weave_xa(LAST, u * HALF, (u + 1) * HALF, nc.vector.tensor_copy)
+            quantise(xb_q[LAST], xb_grouped[LAST], u * HALF, (u + 1) * HALF)
+            hip_scores(LAST, u)
+            quantise(xa_q[LAST], xa_grouped[LAST], u * HALF, (u + 1) * HALF)
+            spine_scores(LAST, u)
         store(0, ())
-        store(1, (0, 2))
+        store(1, (0, N_TILES - 1))

from contextlib import ExitStack

import concourse.mybir as mybir
from concourse.masks import make_identity

K, T, S, PAIRS, H, N = 1024, 4096, 1024, 512, 1536, 384
FLOPS = 2 * K * H * S + 2 * 2 * H * N * PAIRS

F32 = mybir.dt.float32
BF16 = mybir.dt.bfloat16
I32 = mybir.dt.int32
U32 = mybir.dt.uint32
U16 = mybir.dt.uint16
U8 = mybir.dt.uint8
FP8X4 = mybir.dt.float8_e4m3fn_x4
FP4X4 = mybir.dt.float4_e2m1fn_x4
MULT = mybir.AluOpType.mult
ADD = mybir.AluOpType.add
ACT = mybir.ActivationFunctionType

P = 128
PACK = 4
PASS = P * PACK
BANK = 512
K_PASSES = K // PASS
R_PASSES = H // PASS
LAST = R_PASSES - 1
N_TILES = N // P
HALF = PAIRS // 2
LIST_GROUP = 16
QUADS = 4
QUAD = P // QUADS
SCALE_ROWS = 4
GAIN, SLOPE, BEND = 0, 1, 2
FACTOR_ROWS = 3 * R_PASSES

RUN_F32, RUN_BF16 = 2, 4

RAW_BUFS = 4
W_GROUPED_BUFS = 3
W1_MX_BUFS = 2 * K_PASSES
H_BUFS = PACK + 2
STAGE_BANKS = 5
SP_BUFS = PACK + 1
TH_BUFS = PACK
PLANE_BUFS = 2
X_GROUPED_BUFS = 3


def tile_list_spine_hip_scores_kernel(
    tc, tab_words, tab_scales, offs, pos1, pos2, w1, gain, slope, bend, hipm, wsp_words, wsp_scales, whip, shift, out
):
    nc = tc.nc
    with ExitStack() as ctx:
        keep = ctx.enter_context(tc.tile_pool(name="keep", bufs=1))
        ring = ctx.enter_context(tc.tile_pool(name="ring", bufs=2))
        psum = ctx.enter_context(tc.psum_pool(name="psum", bufs=1))

        tab_plane = keep.tile([P, T], U8, name="tab_plane", align_bytes=64)
        wsp_plane = keep.tile([P, R_PASSES, N], U8, name="wsp_plane", align_bytes=64)
        nc.vector.memset(tab_plane[:].bitcast(I32), 0)
        nc.vector.memset(wsp_plane[:].rearrange("p a n -> p (a n)").bitcast(I32), 0)

        idx = keep.tile([P, S // LIST_GROUP], U16, name="idx")
        p1 = keep.tile([P, PAIRS // LIST_GROUP], U16, name="p1")
        p2 = keep.tile([P, PAIRS // LIST_GROUP], U16, name="p2")
        tab = [keep.tile([P, T], U32, name=f"tab{g}") for g in range(K_PASSES)]
        w1_raw = {}
        hip = {}
        whip_raw = {}

        def load_w1(a, g, parts=1):
            width = PASS // parts
            raw = ring.tile([P, parts, PACK, width], F32, name="raw", tag="raw", bufs=RAW_BUFS)
            w1_raw[(a, g)] = raw
            for part in range(parts):
                c0 = a * PASS + part * width
                nc.sync.dma_start(
                    out=raw[:, part],
                    in_=w1[g * PASS : (g + 1) * PASS, c0 : c0 + width].rearrange("(p j) c -> p j c", j=PACK),
                )

        def load_hip(a):
            hip[a] = keep.tile([P, PACK, PAIRS], F32, name=f"hip{a}")
            nc.sync.dma_start(out=hip[a][:], in_=hipm[a * PASS : (a + 1) * PASS].rearrange("(p t) j -> p t j", t=PACK))

        def load_whip(a):
            whip_raw[a] = ring.tile([P, PACK, N], F32, name="raw", tag="raw", bufs=RAW_BUFS)
            nc.sync.dma_start(out=whip_raw[a][:], in_=whip[a * PASS : (a + 1) * PASS].rearrange("(p t) n -> p t n", t=PACK))

        factor_rows = keep.tile([P, PASS], F32, name="factor_rows")
        nc.gpsimd.memset(factor_rows[:], 0.0)
        identity = keep.tile([P, P], F32, name="identity")
        make_identity(nc, identity[:])

        def load_table(g):
            nc.sync.dma_start(out=tab[g][:].bitcast(I32), in_=tab_words[g].rearrange("p t i -> p (t i)").bitcast(I32))

        nc.sync.dma_start(idx[:], offs)
        load_table(0)
        for q in range(QUADS):
            nc.sync.dma_start(
                out=tab_plane[QUAD * q : QUAD * q + SCALE_ROWS * K_PASSES, :].bitcast(I32),
                in_=tab_scales[:, SCALE_ROWS * q : SCALE_ROWS * (q + 1), :].bitcast(I32),
            )
        load_w1(0, 0)
        load_table(1)
        for i, vec in enumerate((gain, slope, bend)):
            nc.sync.dma_start(
                out=factor_rows[R_PASSES * i : R_PASSES * (i + 1), :], in_=vec.rearrange("(a c) -> a c", c=PASS)
            )
        nc.sync.dma_start(out=factor_rows[FACTOR_ROWS : FACTOR_ROWS + N_TILES, :P], in_=shift.rearrange("(c p) -> c p", p=P))
        load_w1(0, 1, parts=2)
        nc.sync.dma_start(p1[:], pos1)
        nc.sync.dma_start(p2[:], pos2)
        load_hip(0)
        load_w1(1, 0)
        load_w1(1, 1)
        wsp_codes = keep.tile([P, R_PASSES, 2 * N], U8, name="wsp_codes", align_bytes=64)
        nc.sync.dma_start(out=wsp_codes[:].bitcast(I32), in_=wsp_words.rearrange("a p c -> p a c").bitcast(I32))
        for q in range(QUADS):
            nc.sync.dma_start(
                out=wsp_plane[QUAD * q : QUAD * q + SCALE_ROWS].bitcast(I32),
                in_=wsp_scales[:, SCALE_ROWS * q : SCALE_ROWS * (q + 1), :].rearrange("a r n -> r a n").bitcast(I32),
            )
        load_hip(1)
        load_w1(2, 0)
        load_w1(2, 1)
        load_whip(0)
        load_hip(2)
        load_whip(1)
        load_whip(2)

        v_plane = keep.tile([P, S], U8, name="v_plane", align_bytes=64)
        nc.vector.tensor_copy(v_plane[:], tab_plane[:].indirect(idx[:]))
        v_codes = []
        for g in range(K_PASSES):
            picked = keep.tile([P, S], U32, name=f"v_codes{g}", align_bytes=64)
            nc.vector.tensor_copy(picked[:], tab[g][:].indirect(idx[:]))
            v_codes.append(picked)

        turned = psum.tile([P, PACK, P], F32, name="turned", tag="scores0")
        for t in range(PACK):
            nc.tensor.transpose(turned[:, t, :], factor_rows[:, t:PASS:PACK], identity[:])
        factors = keep.tile([P, PACK, FACTOR_ROWS], F32, name="factors")
        nc.scalar.copy(factors[:], turned[:, :, :FACTOR_ROWS])

        turned_shift = psum.tile([P, P], F32, name="turned_shift", tag="scores1")
        nc.tensor.transpose(turned_shift[:], factor_rows[:, :P], identity[:])
        shift_c = keep.tile([P, N_TILES], F32, name="shift_c")
        nc.scalar.copy(shift_c[:], turned_shift[:, FACTOR_ROWS : FACTOR_ROWS + N_TILES])

        def factor(i, a, t):
            return factors[:, t, R_PASSES * i + a : R_PASSES * i + a + 1]

        def mx_tiles(width, name, bufs):
            codes = ring.tile([P, width], U32, name=name + "_codes", tag=name + "_codes", bufs=bufs, align_bytes=64)
            plane = ring.tile([P, width], U8, name=name + "_plane", tag=name + "_plane", bufs=bufs, align_bytes=64)
            return codes, plane

        def quantise(mx, grouped, c0, c1):
            nc.vector.quantize_mx(
                out=mx[0][:, c0:c1].bitcast(FP8X4), scales=mx[1][:, c0:c1], in_=grouped[:, PACK * c0 : PACK * c1]
            )

        w1_q = {}

        def prepare_w1(a, g, copies, calls):
            grouped = ring.tile([P, PASS * PACK], BF16, name="w_grouped", tag="w_grouped", bufs=W_GROUPED_BUFS, align_bytes=64)
            dst = grouped[:].rearrange("p (t m j) -> p m j t", t=PACK, j=PACK)
            m_width = P // len(copies)
            for part, pair in enumerate(copies):
                src = w1_raw[(a, g)][:, part].rearrange("p j (m t) -> p m j t", t=PACK)
                for t, copy in zip((0, 2), pair):
                    copy(dst[:, part * m_width : (part + 1) * m_width, :, t : t + 2], src[:, :, :, t : t + 2])
            w1_q[(a, g)] = mx_tiles(PASS, "w1", W1_MX_BUFS)
            for c0 in range(0, PASS, PASS // calls):
                quantise(w1_q[(a, g)], grouped, c0, c0 + PASS // calls)

        def woven(grouped, run, c0, c1):
            return grouped[:, PACK * c0 : PACK * c1].rearrange("p (c i t) -> p c t i", i=run, t=PACK)

        def runs(by_t, run, c0, c1):
            return by_t[:, :, c0:c1].rearrange("p t (c i) -> p c t i", i=run)

        h = {}

        def first_stage(a, t):
            h[(a, t)] = ring.tile([P, S], F32, name="h", tag="h", bufs=H_BUFS)
            for b in range(S // BANK):
                cols = slice(b * BANK, (b + 1) * BANK)
                bank = psum.tile([P, BANK], F32, name="bank", tag="bank", bufs=STAGE_BANKS)
                for g in range(K_PASSES):
                    codes, plane = w1_q[(a, g)]
                    nc.tensor.matmul_mx(
                        out=bank[:],
                        lhsT=codes[:, t * P : (t + 1) * P].bitcast(FP8X4),
                        lhsT_scale=plane[:, t * P : (t + 1) * P],
                        rhs=v_codes[g][:, cols].bitcast(FP8X4),
                        rhs_scale=v_plane[SCALE_ROWS * g : P, cols],
                        start=(g == 0),
                        stop=(g == K_PASSES - 1),
                    )
                if a == 0 and t == 0 and b == 1:
                    nc.vector.tensor_scalar_mul(h[(a, t)][:, cols], bank[:], factor(GAIN, a, t))
                else:
                    nc.scalar.activation(h[(a, t)][:, cols], bank[:], ACT.Copy, scale=factor(GAIN, a, t))

        sp = {}
        th = {}
        xa_by_t = {}
        xb_by_t = {}

        def pick_spine(a, t):
            sp[(a, t)] = ring.tile([P, PAIRS], F32, name="sp", tag="sp", bufs=SP_BUFS)
            nc.vector.tensor_copy(sp[(a, t)][:], h[(a, t)][:].indirect(p1[:]))

        def pick_hip(a, t):
            if t == 0:
                xb_by_t[a] = ring.tile([P, PACK, PAIRS], F32, name="xb_by_t", tag="xb_by_t", bufs=PLANE_BUFS)
            nc.vector.tensor_tensor(xb_by_t[a][:, t, :], h[(a, t)][:].indirect(p2[:]), hip[a][:, t, :], MULT)

        def bent(a, t):
            th[(a, t)] = ring.tile([P, PAIRS], F32, name="th", tag="th", bufs=TH_BUFS)
            nc.scalar.activation(th[(a, t)][:], sp[(a, t)][:], ACT.Tanh, scale=factor(SLOPE, a, t))

        def spine(a, t):
            if t == 0:
                xa_by_t[a] = ring.tile([P, PACK, PAIRS], BF16, name="xa_by_t", tag="xa_by_t", bufs=PLANE_BUFS)
            nc.vector.scalar_tensor_tensor(
                xa_by_t[a][:, t, :], th[(a, t)][:], factor(BEND, a, t), sp[(a, t)][:], MULT, ADD
            )

        xa_grouped = {}
        xb_grouped = {}
        xa_q = {}
        xb_q = {}

        def grouped_tile():
            return ring.tile([P, PAIRS * PACK], BF16, name="x_grouped", tag="x_grouped", bufs=X_GROUPED_BUFS, align_bytes=64)

        def weave_xa(a, c0, c1, copy):
            if c0 == 0:
                xa_grouped[a] = grouped_tile()
                xa_q[a] = mx_tiles(PAIRS, "xa", R_PASSES)
            copy(woven(xa_grouped[a], RUN_BF16, c0, c1), runs(xa_by_t[a], RUN_BF16, c0, c1))

        def weave_xb(a, c0, c1):
            if c0 == 0:
                xb_grouped[a] = grouped_tile()
                xb_q[a] = mx_tiles(PAIRS, "xb", R_PASSES)
            nc.scalar.copy(woven(xb_grouped[a], RUN_F32, c0, c1), runs(xb_by_t[a], RUN_F32, c0, c1))

        whip_q = {}

        def prepare_whip(a):
            grouped = ring.tile([P, N * PACK], BF16, name="w_grouped", tag="w_grouped", bufs=W_GROUPED_BUFS, align_bytes=64)
            nc.scalar.copy(woven(grouped, RUN_F32, 0, N), runs(whip_raw[a], RUN_F32, 0, N))
            whip_q[a] = mx_tiles(N, "whip", R_PASSES)
            quantise(whip_q[a], grouped, 0, N)

        scores = {(0, c): psum.tile([P, HALF], F32, name=f"scores{c}", tag=f"scores{c}") for c in range(N_TILES)}

        def score_pass(u, c, codes, plane, x, start, stop):
            cols = slice(u * HALF, (u + 1) * HALF)
            nc.tensor.matmul_mx(
                out=scores[(u, c)][:],
                lhsT=codes,
                lhsT_scale=plane,
                rhs=x[0][:, cols].bitcast(FP8X4),
                rhs_scale=x[1][:, cols],
                start=start,
                stop=stop,
            )

        def spine_scores(a, u):
            for c in range(N_TILES):
                codes = wsp_codes[:, a, 2 * P * c : 2 * P * (c + 1)].bitcast(FP4X4)
                score_pass(u, c, codes, wsp_plane[:, a, P * c : P * (c + 1)], xa_q[a], a == 0, a == LAST)

        def hip_scores(a, u):
            for c in range(N_TILES):
                codes = whip_q[a][0][:, P * c : P * (c + 1)].bitcast(FP8X4)
                score_pass(u, c, codes, whip_q[a][1][:, P * c : P * (c + 1)], xb_q[a], False, False)

        def store(u, on_vector):
            for c in range(N_TILES):
                res = ring.tile([P, HALF], F32, name="res", tag="res", bufs=2 * N_TILES)
                if c in on_vector:
                    nc.vector.tensor_scalar_add(res[:], scores[(u, c)][:], shift_c[:, c : c + 1])
                else:
                    nc.scalar.activation(res[:], scores[(u, c)][:], ACT.Identity, bias=shift_c[:, c : c + 1])
                nc.sync.dma_start(out=out[c * P : (c + 1) * P, u * HALF : (u + 1) * HALF], in_=res[:])

        on_scalar = [(nc.scalar.copy, nc.scalar.copy)]
        prepare_w1(0, 0, on_scalar, 1)
        prepare_w1(0, 1, on_scalar + [(nc.vector.tensor_copy, nc.scalar.copy)], 2)

        for a in range(R_PASSES):
            for t in range(PACK):
                first_stage(a, t)
                pick_spine(a, t)
                if t >= 1:
                    bent(a, t - 1)
                pick_hip(a, t)
                if a < LAST and 1 <= t <= K_PASSES:
                    prepare_w1(a + 1, t - 1, on_scalar, 1)
                if a == LAST and t < R_PASSES:
                    prepare_whip(t)
                if t >= 1:
                    spine(a, t - 1)
                if a > 0 and t == 0:
                    weave_xa(a - 1, 0, HALF, nc.scalar.copy)
                    weave_xa(a - 1, HALF, PAIRS, nc.vector.tensor_copy)
                    quantise(xa_q[a - 1], xa_grouped[a - 1], 0, PAIRS)
                    spine_scores(a - 1, 0)
                if a > 0 and t == PACK - 1:
                    weave_xb(a - 1, 0, PAIRS)
                    quantise(xb_q[a - 1], xb_grouped[a - 1], 0, PAIRS)
            bent(a, PACK - 1)
            spine(a, PACK - 1)

        for c in range(N_TILES):
            scores[(1, c)] = psum.tile([P, HALF], F32, name="bank", tag="bank", bufs=STAGE_BANKS)
        for a in range(LAST):
            hip_scores(a, 0)
        for a in range(LAST):
            spine_scores(a, 1)
            hip_scores(a, 1)

        for u in range(2):
            weave_xb(LAST, u * HALF, (u + 1) * HALF)
        for u in range(2):
            weave_xa(LAST, u * HALF, (u + 1) * HALF, nc.vector.tensor_copy)
            quantise(xb_q[LAST], xb_grouped[LAST], u * HALF, (u + 1) * HALF)
            hip_scores(LAST, u)
            quantise(xa_q[LAST], xa_grouped[LAST], u * HALF, (u + 1) * HALF)
            spine_scores(LAST, u)
        store(0, ())
        store(1, (0, N_TILES - 1))
